import numpy as np
import ml_dtypes


def mxq(x, axis, fmt="e4m3"):
    dtype, down = {"e4m3": (ml_dtypes.float8_e4m3fn, 7), "e5m2": (ml_dtypes.float8_e5m2, 14)}[fmt]
    v = np.moveaxis(np.asarray(x, np.float32).astype(ml_dtypes.bfloat16).astype(np.float64), axis, -1)
    blocks = v.reshape(v.shape[:-1] + (-1, 32))
    amax = np.abs(blocks).max(-1, keepdims=True)
    byte = np.maximum(np.where(amax > 0, np.frexp(amax)[1] - 1 + 127, 0) - down, 1)
    scale = np.exp2(byte - 127.0)
    codes = (blocks / scale).astype(np.float32).astype(dtype).astype(np.float64)
    return np.moveaxis((codes * scale).reshape(v.shape), -1, axis)


WIDE = False


def mx_kscale(k):
    if not WIDE:
        return np.ones(k)
    levels = np.array([10, -10, 5, -5, 0])
    if k % 512:
        return np.exp2(np.random.permutation(np.resize(levels, k // 32))).repeat(32)
    a = np.empty((k // 512, 16))
    for p in range(k // 512):
        a[p, :8] = np.random.permutation(np.resize(levels, 8))
        for g in range(8):
            far = levels[np.abs(levels - a[p, g]) >= 10]
            a[p, g + 8] = far[np.random.randint(len(far))]
    return np.exp2(a.ravel()).repeat(32)


def f64(x):
    return np.asarray(x).astype(np.float64)


def striped(idx):
    return np.tile(idx.reshape(-1, 16).T, (8, 1)).astype(np.uint16)


def unstriped(offs):
    return offs[:16].T.reshape(-1).astype(np.int64)


E2M1 = np.array([0.0, 0.5, 1.0, 1.5, 2.0, 3.0, 4.0, 6.0, -0.0, -0.5, -1.0, -1.5, -2.0, -3.0, -4.0, -6.0])


def pack_weight(w, fmt):
    k, n = w.shape
    w = f64(np.asarray(w, np.float32).astype(ml_dtypes.bfloat16)).reshape(k // 32, 32, n)
    amax = np.abs(w).max(1)
    if fmt == "e4m3":
        byte = np.frexp(amax)[1] - 1 + 127 - 7
    else:
        mant, ex = np.frexp(amax / 6.0)
        byte = np.where(mant > 0.5, ex, ex - 1) + 127
    byte = np.clip(np.where(amax > 0, byte, 1), 1, 254)
    scaled = (w * np.exp2(127.0 - byte)[:, None, :]).reshape(k, n).astype(np.float32)
    by_word = np.ascontiguousarray(scaled.reshape(k // 512, 128, 4, n).transpose(0, 1, 3, 2))
    if fmt == "e4m3":
        words = by_word.astype(ml_dtypes.float8_e4m3fn).view(np.uint8)
    else:
        c = by_word.astype(ml_dtypes.float4_e2m1fn).view(np.uint8) & 0xF
        words = (c[..., 0::2] | (c[..., 1::2] << 4)).reshape(k // 512, 128, 2 * n)
    return np.ascontiguousarray(words), np.ascontiguousarray(byte.astype(np.uint8).reshape(k // 512, 16, n))


def unpack_weight(words, scales, fmt):
    g, _, n = scales.shape
    words = np.ascontiguousarray(words).reshape(g, 128, n, -1)
    if fmt == "e4m3":
        vals = words.view(ml_dtypes.float8_e4m3fn).astype(np.float64)
    else:
        nib = np.empty((g, 128, n, 4), np.uint8)
        nib[..., 0::2] = words & 0xF
        nib[..., 1::2] = words >> 4
        vals = E2M1[nib]
    vals = vals * np.repeat(np.exp2(scales.astype(np.float64) - 127.0), 8, axis=1)[..., None]
    return vals.transpose(0, 1, 3, 2).reshape(g * 512, n)


def gelu(v):
    return 0.5 * v * (1.0 + np.tanh(np.sqrt(2.0 / np.pi) * (v + 0.044715 * v**3)))


K, H, T, S, T2, T3, S2, P = 512, 1024, 2048, 1024, 2048, 2048, 1024, 512


def setup_inputs():
    n = np.random.standard_normal
    s = mx_kscale(K)[:, None]
    u = mx_kscale(H)[:, None]
    tab_words, tab_scales = pack_weight(n((K, T)) * s, "e4m3")
    tab2_words, tab2_scales = pack_weight(n((H, T3)) / np.sqrt(H) / u, "e4m3")
    wb_words, wb_scales = pack_weight(n((K, H)) / np.sqrt(K) / s * u.T, "e4m3")
    wc_words, wc_scales = pack_weight(n((K, H)) / np.sqrt(K) / s * u.T, "e2m1")
    return {
        "tab_words": tab_words, "tab_scales": tab_scales,
        "tab2_words": tab2_words, "tab2_scales": tab2_scales,
        "wa": (n((K, H)) / np.sqrt(K) / s * u.T).astype(np.float32),
        "wb_words": wb_words, "wb_scales": wb_scales,
        "wc_words": wc_words, "wc_scales": wc_scales,
        "wgs": np.exp(0.3 * n((128, S))).astype(np.float32),
        "page0": (n((H, T2)) * u).astype(np.float32),
        "shift": (0.7 * n(H) * u[:, 0]).astype(np.float32),
        "subj": n((S2, P)).astype(np.float32),
        "cand": (0.5 * n(S2)).astype(np.float32),
        "offs": striped(np.random.permutation(T)[:S]),
        "offs2": striped(np.random.permutation(T3)[:S2]),
        "offs3": striped(np.random.permutation(T2)[:S]),
        "offs4": striped(np.random.permutation(T2)[:P]),
    }


def reference(tab_words, tab_scales, tab2_words, tab2_scales, wa, wb_words, wb_scales, wc_words, wc_scales,
              wgs, page0, shift, subj, cand, offs, offs2, offs3, offs4):
    v = unpack_weight(tab_words, tab_scales, "e4m3")[:, unstriped(offs)]
    v2 = unpack_weight(tab2_words, tab2_scales, "e4m3")[:, unstriped(offs2)]
    ya = mxq(f64(wa), 0, "e4m3").T @ v
    yb = unpack_weight(wb_words, wb_scales, "e4m3").T @ v
    yc = unpack_weight(wc_words, wc_scales, "e2m1").T @ v
    h = np.minimum(np.maximum(ya, yb), yc)
    page = f64(page0).copy()
    page[:, unstriped(offs3)] = np.tile(f64(wgs), (H // 128, 1)) * h
    x = page[:, unstriped(offs4)] + f64(shift)[:, None]
    e = v2.T @ mxq(x, 0, "e4m3")
    return np.tanh(e) * f64(subj) + f64(cand)[:, None]

@@ -1,0 +1,226 @@
+from contextlib import ExitStack
+
+import concourse.mybir as mybir
+from concourse.masks import make_identity
+
+K, H, T, S, T2, T3, S2, NX = 512, 1024, 2048, 1024, 2048, 2048, 1024, 512
+FLOPS = 3 * 2 * K * H * S + 2 * H * S2 * NX
+
+F32 = mybir.dt.float32
+BF16 = mybir.dt.bfloat16
+I32 = mybir.dt.int32
+U32 = mybir.dt.uint32
+U16 = mybir.dt.uint16
+U8 = mybir.dt.uint8
+FP8X4 = mybir.dt.float8_e4m3fn_x4
+FP4X4 = mybir.dt.float4_e2m1fn_x4
+ALU = mybir.AluOpType
+ACT = mybir.ActivationFunctionType
+
+P = 128
+PACK = 4
+HALF = 512
+
+
+def tile_list_catalogue_related_scores_kernel(
+    tc, tab_words, tab_scales, tab2_words, tab2_scales, wa, wb_words, wb_scales, wc_words, wc_scales,
+    wgs, page0, shift, subj, cand, offs, offs2, offs3, offs4, out,
+):
+    nc = tc.nc
+    with ExitStack() as ctx:
+        keep = ctx.enter_context(tc.tile_pool(name="keep", bufs=1))
+        ring = ctx.enter_context(tc.tile_pool(name="ring", bufs=2))
+        psum = ctx.enter_context(tc.psum_pool(name="psum", bufs=2))
+
+        def kept(shape, dtype, name, tag=""):
+            return keep.tile(shape, dtype, name=name, tag=tag or name, align_bytes=64)
+
+        list_v = kept([P, S // 16], U16, "list_v")
+        list_v2 = kept([P, S2 // 16], U16, "list_v2")
+        list_put = kept([P, S // 16], U16, "list_put")
+        list_get = kept([P, NX // 16], U16, "list_get")
+        tab_w = kept([P, T], I32, "tab_w")
+        tab_s = kept([P, T], U8, "tab_s")
+        tab2_w = [kept([P, T3], I32, f"tab2_w{a}") for a in range(2)]
+        tab2_s = kept([P, T3], U8, "tab2_s")
+        wa_raw = [kept([P, PACK, HALF], F32, f"wa_raw{a}") for a in range(2)]
+        wa_bf = [kept([P, HALF, PACK], BF16, f"wa_bf{a}") for a in range(2)]
+        wa_w = [kept([P, HALF], U32, f"wa_w{a}") for a in range(2)]
+        wa_s = [kept([P, HALF], U8, f"wa_s{a}") for a in range(2)]
+        wb_w = [kept([P, HALF], I32, f"wb_w{a}") for a in range(2)]
+        wc_w = [kept([P, 2 * HALF], U8, f"wc_w{a}") for a in range(2)]
+        wb_s = kept([P, H], U8, "wb_s")
+        wc_s = kept([P, H], U8, "wc_s")
+        factor = [kept([P, PACK, HALF], F32, f"factor{jh}") for jh in range(2)]
+        page = [[kept([P, T2], F32, f"page{a}_{t}") for t in range(PACK)] for a in range(2)]
+        shift_sb = kept([P, 2, PACK], F32, "shift_sb")
+        cand_sb = kept([P, S2 // P], F32, "cand_sb")
+        v_w = [kept([P, HALF], U32, f"v_w{jh}") for jh in range(2)]
+        v_s = [kept([P, HALF], U8, f"v_s{jh}") for jh in range(2)]
+        v2_w = [kept([P, S2], U32, f"v2_w{a}") for a in range(2)]
+        v2_s = kept([P, S2], U8, "v2_s")
+        x_bf = [kept([P, NX, PACK], BF16, f"x_bf{a}") for a in range(2)]
+        x_w = [kept([P, NX], U32, f"x_w{a}") for a in range(2)]
+        x_s = [kept([P, NX], U8, f"x_s{a}") for a in range(2)]
+        ident = kept([P, P], F32, "ident")
+
+        def load_scale_rows(queue, plane, scales):
+            passes = scales.shape[0]
+            for q in range(4):
+                rows = scales[:, 4 * q : 4 * q + 4, :]
+                if passes == 1:
+                    rows = rows[0]
+                queue.dma_start(out=plane[32 * q : 32 * q + 4 * passes, :].bitcast(I32), in_=rows.bitcast(I32))
+
+        def words(dram, a, c0, c1):
+            return dram[a].rearrange("p c i -> p (c i)")[:, 4 * c0 : 4 * c1].bitcast(I32)
+
+        def load_weights(a):
+            cols = slice(HALF * a, HALF * (a + 1))
+            nc.sync.dma_start(out=wa_raw[a][:], in_=wa.rearrange("(p i) r -> p i r", i=PACK)[:, :, cols])
+            nc.sync.dma_start(out=wb_w[a][:], in_=words(wb_words, 0, cols.start, cols.stop))
+            nc.sync.dma_start(out=wc_w[a][:].bitcast(I32), in_=wc_words[0][:, 2 * cols.start : 2 * cols.stop].bitcast(I32))
+
+        def load_factor(jh):
+            rows = wgs.rearrange("(q t) j -> q t j", t=PACK)[:, :, HALF * jh : HALF * (jh + 1)]
+            for quad in range(4):
+                nc.sync.dma_start(out=factor[jh][32 * quad : 32 * (quad + 1)], in_=rows)
+
+        def load_page(a, t):
+            rows = page0.rearrange("(a p t) c -> a t p c", a=2, t=PACK)[a, t]
+            nc.sync.dma_start(out=page[a][t][:], in_=rows)
+
+        nc.vector.memset(tab_s[:].bitcast(I32), 0)
+        nc.vector.memset(wb_s[:].bitcast(I32), 0)
+        nc.gpsimd.memset(wc_s[:].bitcast(I32), 0)
+        nc.sync.dma_start(list_v[:], offs)
+        nc.sync.dma_start(out=tab_w[:], in_=words(tab_words, 0, 0, T))
+        load_scale_rows(nc.sync, tab_s, tab_scales)
+        load_scale_rows(nc.gpsimd, wc_s, wc_scales)
+        make_identity(nc, ident[:])
+        nc.gpsimd.memset(tab2_s[:].bitcast(I32), 0)
+        load_weights(0)
+        load_scale_rows(nc.sync, wb_s, wb_scales)
+        nc.sync.dma_start(list_put[:], offs3)
+        load_factor(0)
+        for t in range(PACK):
+            load_page(0, t)
+        load_factor(1)
+        load_weights(1)
+        nc.sync.dma_start(list_get[:], offs4)
+        with nc.allow_non_contiguous_dma(reason="small per-partition vectors"):
+            nc.sync.dma_start(out=shift_sb[:], in_=shift.rearrange("(a p t) -> p a t", a=2, t=PACK))
+        nc.sync.dma_start(list_v2[:], offs2)
+        load_scale_rows(nc.sync, tab2_s, tab2_scales)
+        for a in range(2):
+            nc.sync.dma_start(out=tab2_w[a][:], in_=words(tab2_words, a, 0, T3))
+        for t in range(PACK):
+            load_page(1, t)
+        with nc.allow_non_contiguous_dma(reason="small per-partition vectors"):
+            nc.sync.dma_start(out=cand_sb[:], in_=cand.rearrange("(c p) -> p c", p=P))
+
+        def gather_v(jh):
+            entries = list_v[:, 32 * jh : 32 * (jh + 1)]
+            nc.vector.tensor_copy(v_w[jh][:], tab_w[:].bitcast(U32).indirect(entries))
+            nc.vector.tensor_copy(v_s[jh][:], tab_s[:].indirect(entries))
+
+        def interleave_wa(a, copy):
+            copy(wa_bf[a][:].rearrange("p (c i) t -> p c t i", i=4), wa_raw[a][:].rearrange("p t (c i) -> p c t i", i=4))
+
+        def quantise(codes, scales, values):
+            nc.vector.quantize_mx(out=codes[:].bitcast(FP8X4), scales=scales[:], in_=values[:].rearrange("p c t -> p (c t)"))
+
+        def dealt(bank):
+            return bank[:].rearrange("p (m t) -> p t m", t=PACK)
+
+        def features(a, jh, jb, h_rows):
+            entries = slice(P * jb, P * (jb + 1))
+            cols = slice(HALF * a, HALF * (a + 1))
+            ya = psum.tile([P, HALF], F32, name="ya", tag="ya")
+            yb = psum.tile([P, HALF], F32, name="yb", tag="yb")
+            yc = psum.tile([P, HALF], F32, name="yc", tag="yc")
+            for bank, codes, scales in (
+                (ya, wa_w[a][:].bitcast(FP8X4), wa_s[a][:]),
+                (yb, wb_w[a][:].bitcast(FP8X4), wb_s[:, cols]),
+                (yc, wc_w[a][:].bitcast(FP4X4), wc_s[:, cols]),
+            ):
+                nc.tensor.matmul_mx(
+                    out=bank[:], lhsT=v_w[jh][:, entries].bitcast(FP8X4), lhsT_scale=v_s[jh][:, entries],
+                    rhs=codes, rhs_scale=scales, start=True, stop=True,
+                )
+            ya_sb = ring.tile([P, PACK, P], F32, name="ya_sb")
+            larger = ring.tile([P, PACK, P], F32, name="larger")
+            h_entries = ring.tile([P, PACK, P], F32, name="h_entries")
+            nc.scalar.copy(ya_sb[:], dealt(ya))
+            nc.vector.tensor_tensor(larger[:], dealt(yb), ya_sb[:], ALU.max)
+            nc.vector.tensor_tensor(h_entries[:], dealt(yc), larger[:], ALU.min)
+            turned = psum.tile([P, PACK, P], F32, name="turned", tag="turned")
+            for t in range(PACK):
+                nc.tensor.transpose(turned[:, t, :], h_entries[:, t, :], ident[:])
+            nc.scalar.copy(h_rows[:, :, entries], turned[:])
+
+        def put(a, jh, t, h_rows):
+            entries = list_put[:, 32 * jh : 32 * (jh + 1)]
+            nc.vector.tensor_tensor(page[a][t][:].indirect(entries), h_rows[:, t, :], factor[jh][:, t, :], ALU.mult)
+
+        def fetch(a, t):
+            picked = ring.tile([P, NX], F32, name="picked")
+            nc.vector.tensor_copy(picked[:], page[a][t][:].indirect(list_get[:]))
+            nc.scalar.activation(x_bf[a][:, :, t], picked[:], ACT.Identity, bias=shift_sb[:, a, t : t + 1])
+
+        def gather_v2():
+            for a in range(2):
+                nc.vector.tensor_copy(v2_w[a][:], tab2_w[a][:].bitcast(U32).indirect(list_v2[:]))
+            nc.vector.tensor_copy(v2_s[:], tab2_s[:].indirect(list_v2[:]))
+
+        gather_v(0)
+        interleave_wa(0, nc.vector.tensor_copy)
+        gather_v(1)
+        quantise(wa_w[0], wa_s[0], wa_bf[0])
+        interleave_wa(1, nc.scalar.copy)
+
+        subj_sb = []
+        groups = [(a, jh) for a in range(2) for jh in range(2)]
+        h_rows = {}
+        h_rows[0] = ring.tile([P, PACK, HALF], F32, name="h_rows")
+        for jb in range(4):
+            features(0, 0, jb, h_rows[0])
+        for g, (a, jh) in enumerate(groups):
+            if g + 1 < len(groups):
+                h_rows[g + 1] = ring.tile([P, PACK, HALF], F32, name="h_rows")
+            if g == 1:
+                quantise(wa_w[1], wa_s[1], wa_bf[1])
+            if g == 2:
+                for i in range(2):
+                    subj_sb.append(kept([P, 4, NX], F32, f"subj{i}", tag=f"wa_raw{i}"))
+                    nc.sync.dma_start(out=subj_sb[i][:], in_=subj.rearrange("(i c p) n -> i p c n", i=2, p=P)[i])
+                quantise(x_w[0], x_s[0], x_bf[0])
+                gather_v2()
+            for t in range(PACK):
+                put(a, jh, t, h_rows[g])
+                if jh == 1:
+                    fetch(a, t)
+                if g + 1 < len(groups):
+                    features(*groups[g + 1], t, h_rows[g + 1])
+        quantise(x_w[1], x_s[1], x_bf[1])
+
+        tags = ("ya", "yb", "yc", "turned")
+        scores = [psum.tile([P, NX], F32, name=f"score{m}", tag=tags[m % 4]) for m in range(S2 // P)]
+        for a in range(2):
+            for m in range(S2 // P):
+                cands = slice(P * m, P * (m + 1))
+                nc.tensor.matmul_mx(
+                    out=scores[m][:], lhsT=v2_w[a][:, cands].bitcast(FP8X4), lhsT_scale=v2_s[4 * a :, cands],
+                    rhs=x_w[a][:].bitcast(FP8X4), rhs_scale=x_s[a][:], start=(a == 0), stop=(a == 1),
+                )
+        for m in range(S2 // P):
+            squashed = ring.tile([P, NX], F32, name="squashed", bufs=4)
+            weighted = ring.tile([P, NX], F32, name="weighted", bufs=4)
+            result = ring.tile([P, NX], F32, name="result", bufs=4)
+            nc.scalar.activation(squashed[:], scores[m][:], ACT.Tanh)
+            nc.vector.tensor_tensor(weighted[:], squashed[:], subj_sb[m // 4][:, m % 4, :], ALU.mult)
+            if m % 3 == 1:
+                nc.scalar.activation(result[:], weighted[:], ACT.Identity, bias=cand_sb[:, m : m + 1])
+            else:
+                nc.vector.tensor_scalar(result[:], weighted[:], cand_sb[:, m : m + 1], None, ALU.add)
+            nc.sync.dma_start(out=out[P * m : P * (m + 1), :], in_=result[:])

@@ -20,6 +20,15 @@ ACT = mybir.ActivationFunctionType
 P = 128
 PACK = 4
 HALF = 512
+QUARTER = 256
+V_CUTS = (0, 256, 512, 1024)
+FACTOR_CUTS = (0, 256, 512, 1024)
+LAG = 2
+LARGER = 6
+HB = 3
+WA_AT = 2
+LATER = {WA_AT: "wa_bf2", WA_AT + 1: "wa_bf3", 5: "v2_s", 6: "v2_w0", 7: "v2_w1"}
+VECTOR_BLOCKS = 2
 
 
 def tile_list_catalogue_related_scores_kernel(
@@ -44,23 +53,23 @@ def tile_list_catalogue_related_scores_kernel(
         tab2_w = [kept([P, T3], I32, f"tab2_w{a}") for a in range(2)]
         tab2_s = kept([P, T3], U8, "tab2_s")
         wa_raw = [kept([P, PACK, HALF], F32, f"wa_raw{a}") for a in range(2)]
-        wa_bf = [kept([P, HALF, PACK], BF16, f"wa_bf{a}") for a in range(2)]
+        wa_bf = {q: kept([P, QUARTER, PACK], BF16, f"wa_bf{q}") for q in range(2)}
         wa_w = [kept([P, HALF], U32, f"wa_w{a}") for a in range(2)]
         wa_s = [kept([P, HALF], U8, f"wa_s{a}") for a in range(2)]
         wb_w = [kept([P, HALF], I32, f"wb_w{a}") for a in range(2)]
         wc_w = [kept([P, 2 * HALF], U8, f"wc_w{a}") for a in range(2)]
         wb_s = kept([P, H], U8, "wb_s")
         wc_s = kept([P, H], U8, "wc_s")
-        factor = [kept([P, PACK, HALF], F32, f"factor{jh}") for jh in range(2)]
+        factor = [kept([P, PACK, hi - lo], F32, f"factor{lo}") for lo, hi in zip(FACTOR_CUTS, FACTOR_CUTS[1:])]
         page = [[kept([P, T2], F32, f"page{a}_{t}") for t in range(PACK)] for a in range(2)]
         shift_sb = kept([P, 2, PACK], F32, "shift_sb")
         cand_sb = kept([P, S2 // P], F32, "cand_sb")
-        v_w = [kept([P, HALF], U32, f"v_w{jh}") for jh in range(2)]
-        v_s = [kept([P, HALF], U8, f"v_s{jh}") for jh in range(2)]
-        v2_w = [kept([P, S2], U32, f"v2_w{a}") for a in range(2)]
-        v2_s = kept([P, S2], U8, "v2_s")
-        x_bf = [kept([P, NX, PACK], BF16, f"x_bf{a}") for a in range(2)]
-        x_w = [kept([P, NX], U32, f"x_w{a}") for a in range(2)]
+        v_w = {}
+        v_s = {}
+        v2_w = {}
+        v2_s = {}
+        x_bf = {}
+        x_w = {}
         x_s = [kept([P, NX], U8, f"x_s{a}") for a in range(2)]
         ident = kept([P, P], F32, "ident")
 
@@ -81,10 +90,10 @@ def tile_list_catalogue_related_scores_kernel(
             nc.sync.dma_start(out=wb_w[a][:], in_=words(wb_words, 0, cols.start, cols.stop))
             nc.sync.dma_start(out=wc_w[a][:].bitcast(I32), in_=wc_words[0][:, 2 * cols.start : 2 * cols.stop].bitcast(I32))
 
-        def load_factor(jh):
-            rows = wgs.rearrange("(q t) j -> q t j", t=PACK)[:, :, HALF * jh : HALF * (jh + 1)]
-            for quad in range(4):
-                nc.sync.dma_start(out=factor[jh][32 * quad : 32 * (quad + 1)], in_=rows)
+        def load_factor(c):
+            rows = wgs.rearrange("(q t) j -> q t j", t=PACK)[:, :, FACTOR_CUTS[c] : FACTOR_CUTS[c + 1]]
+            for quad in (0, 2, 1, 3):
+                nc.sync.dma_start(out=factor[c][32 * quad : 32 * (quad + 1)], in_=rows)
 
         def load_page(a, t):
             rows = page0.rearrange("(a p t) c -> a t p c", a=2, t=PACK)[a, t]
@@ -92,20 +101,22 @@ def tile_list_catalogue_related_scores_kernel(
 
         nc.vector.memset(tab_s[:].bitcast(I32), 0)
         nc.vector.memset(wb_s[:].bitcast(I32), 0)
+        nc.vector.memset(tab2_s[:].bitcast(I32), 0)
         nc.gpsimd.memset(wc_s[:].bitcast(I32), 0)
         nc.sync.dma_start(list_v[:], offs)
         nc.sync.dma_start(out=tab_w[:], in_=words(tab_words, 0, 0, T))
         load_scale_rows(nc.sync, tab_s, tab_scales)
         load_scale_rows(nc.gpsimd, wc_s, wc_scales)
         make_identity(nc, ident[:])
-        nc.gpsimd.memset(tab2_s[:].bitcast(I32), 0)
         load_weights(0)
         load_scale_rows(nc.sync, wb_s, wb_scales)
+        load_page(0, 0)
         nc.sync.dma_start(list_put[:], offs3)
         load_factor(0)
-        for t in range(PACK):
+        for t in range(1, PACK):
             load_page(0, t)
         load_factor(1)
+        load_factor(2)
         load_weights(1)
         nc.sync.dma_start(list_get[:], offs4)
         with nc.allow_non_contiguous_dma(reason="small per-partition vectors"):
@@ -119,90 +130,171 @@ def tile_list_catalogue_related_scores_kernel(
         with nc.allow_non_contiguous_dma(reason="small per-partition vectors"):
             nc.sync.dma_start(out=cand_sb[:], in_=cand.rearrange("(c p) -> p c", p=P))
 
-        def gather_v(jh):
-            entries = list_v[:, 32 * jh : 32 * (jh + 1)]
-            nc.vector.tensor_copy(v_w[jh][:], tab_w[:].bitcast(U32).indirect(entries))
-            nc.vector.tensor_copy(v_s[jh][:], tab_s[:].indirect(entries))
+        def gather_words(c, tag=""):
+            v_w[c] = kept([P, V_CUTS[c + 1] - V_CUTS[c]], U32, f"v_w{c}", tag)
+            nc.vector.tensor_copy(v_w[c][:], tab_w[:].bitcast(U32).indirect(list_v[:, V_CUTS[c] // 16 : V_CUTS[c + 1] // 16]))
 
-        def interleave_wa(a, copy):
-            copy(wa_bf[a][:].rearrange("p (c i) t -> p c t i", i=4), wa_raw[a][:].rearrange("p t (c i) -> p c t i", i=4))
+        def gather_scales(c, tag=""):
+            v_s[c] = kept([P, V_CUTS[c + 1] - V_CUTS[c]], U8, f"v_s{c}", tag)
+            nc.vector.tensor_copy(v_s[c][:], tab_s[:].indirect(list_v[:, V_CUTS[c] // 16 : V_CUTS[c + 1] // 16]))
+
+        def interleave_wa(q, copy):
+            raw = wa_raw[q // 2][:, :, QUARTER * (q % 2) : QUARTER * (q % 2 + 1)]
+            copy(wa_bf[q][:].rearrange("p (c i) t -> p c t i", i=4), raw.rearrange("p t (c i) -> p c t i", i=4))
+
+        def quantise_wa(q):
+            cols = slice(QUARTER * (q % 2), QUARTER * (q % 2 + 1))
+            quantise(wa_w[q // 2][:, cols], wa_s[q // 2][:, cols], wa_bf[q])
+
+        def cut_of(cuts, entry):
+            c = max(i for i, lo in enumerate(cuts[:-1]) if lo <= entry)
+            return c, entry - cuts[c]
 
         def quantise(codes, scales, values):
-            nc.vector.quantize_mx(out=codes[:].bitcast(FP8X4), scales=scales[:], in_=values[:].rearrange("p c t -> p (c t)"))
+            nc.vector.quantize_mx(out=codes.bitcast(FP8X4), scales=scales, in_=values[:].rearrange("p c t -> p (c t)"))
+
+        def step(shape, tag):
+            return ring.tile(shape, F32, name=tag, tag=tag, bufs={"larger": LARGER, "excess": 4, "h_rows": HB}.get(tag, 3))
 
         def dealt(bank):
             return bank[:].rearrange("p (m t) -> p t m", t=PACK)
 
-        def features(a, jh, jb, h_rows):
-            entries = slice(P * jb, P * (jb + 1))
-            cols = slice(HALF * a, HALF * (a + 1))
-            ya = psum.tile([P, HALF], F32, name="ya", tag="ya")
-            yb = psum.tile([P, HALF], F32, name="yb", tag="yb")
-            yc = psum.tile([P, HALF], F32, name="yc", tag="yc")
-            for bank, codes, scales in (
-                (ya, wa_w[a][:].bitcast(FP8X4), wa_s[a][:]),
-                (yb, wb_w[a][:].bitcast(FP8X4), wb_s[:, cols]),
-                (yc, wc_w[a][:].bitcast(FP4X4), wc_s[:, cols]),
-            ):
-                nc.tensor.matmul_mx(
-                    out=bank[:], lhsT=v_w[jh][:, entries].bitcast(FP8X4), lhsT_scale=v_s[jh][:, entries],
-                    rhs=codes, rhs_scale=scales, start=True, stop=True,
-                )
-            ya_sb = ring.tile([P, PACK, P], F32, name="ya_sb")
-            larger = ring.tile([P, PACK, P], F32, name="larger")
-            h_entries = ring.tile([P, PACK, P], F32, name="h_entries")
-            nc.scalar.copy(ya_sb[:], dealt(ya))
-            nc.vector.tensor_tensor(larger[:], dealt(yb), ya_sb[:], ALU.max)
-            nc.vector.tensor_tensor(h_entries[:], dealt(yc), larger[:], ALU.min)
-            turned = psum.tile([P, PACK, P], F32, name="turned", tag="turned")
-            for t in range(PACK):
-                nc.tensor.transpose(turned[:, t, :], h_entries[:, t, :], ident[:])
-            nc.scalar.copy(h_rows[:, :, entries], turned[:])
+        blocks = [(a, block) for a in range(2) for block in range(S // P)]
+        terms = {}
+        picked = {}
+        neg_larger = {}
+        h_rows = {}
 
-        def put(a, jh, t, h_rows):
-            entries = list_put[:, 32 * jh : 32 * (jh + 1)]
-            nc.vector.tensor_tensor(page[a][t][:].indirect(entries), h_rows[:, t, :], factor[jh][:, t, :], ALU.mult)
+        def product(n, tag, codes, scales):
+            c, first = cut_of(V_CUTS, P * blocks[n][1])
+            entries = slice(first, first + P)
+            bank = psum.tile([P, HALF], F32, name=tag, tag=tag)
+            nc.tensor.matmul_mx(
+                out=bank[:], lhsT=v_w[c][:, entries].bitcast(FP8X4), lhsT_scale=v_s[c][:, entries],
+                rhs=codes, rhs_scale=scales, start=True, stop=True,
+            )
+            return dealt(bank)
+
+        def maximum(n):
+            a = blocks[n][0]
+            ya = product(n, "ya", wa_w[a][:].bitcast(FP8X4), wa_s[a][:])
+            yb = product(n, "yb", wb_w[a][:].bitcast(FP8X4), wb_s[:, HALF * a : HALF * (a + 1)])
+            neg_ya = kept([P, PACK, P], F32, "first_ya") if n == 1 else step([P, PACK, P], "ya_sb")
+            neg_larger[n] = step([P, PACK, P], "larger")
+            nc.scalar.activation(neg_ya[:], ya, ACT.Copy, scale=-1.0)
+            nc.vector.scalar_tensor_tensor(neg_larger[n][:], yb, -1.0, neg_ya[:], ALU.mult, ALU.min)
+
+        def minimum(n):
+            a = blocks[n][0]
+            yc = product(n, "turned" if n in (2, 3) else "yc", wc_w[a][:].bitcast(FP4X4), wc_s[:, HALF * a : HALF * (a + 1)])
+            excess = step([P, PACK, P], "excess")
+            if n < VECTOR_BLOCKS:
+                nc.vector.scalar_tensor_tensor(excess[:], yc, -1.0, neg_larger[n][:], ALU.mult, ALU.max)
+                terms[n] = [excess]
+            else:
+                yc_sb = step([P, PACK, P], "yc_sb")
+                room = step([P, PACK, P], "room")
+                nc.scalar.copy(yc_sb[:], yc)
+                nc.gpsimd.tensor_tensor(room[:], yc_sb[:], neg_larger[n][:], ALU.add)
+                nc.scalar.activation(excess[:], room[:], ACT.Relu, scale=-1.0)
+                terms[n] = [neg_larger[n], excess]
+
+        def turn(n):
+            a, block = blocks[n]
+            piece, pair = block // 2, block % 2
+            turned = psum.tile([P, 2, 2 * P], F32, name="turned", tag="turned")
+            passes = [(side, term, i) for side in range(2) for term in terms[n - pair + side] for i in range(2)]
+            for k, (side, term, i) in enumerate(passes):
+                nc.tensor.matmul(
+                    turned[:, i, P * side : P * (side + 1)], term[:, 2 * pair + i, :], ident[:], is_transpose=True,
+                    start=(k == 0), stop=(k == len(passes) - 1),
+                )
+            h_block = step([P, 2, 2 * P], "h_block")
+            nc.scalar.activation(h_block[:], turned[:], ACT.Copy, scale=-1.0)
+            h_rows[n] = kept([P, 2, 2 * P], F32, f"h_rows{n}", LATER[n]) if n in LATER else step([P, 2, 2 * P], "h_rows")
+            c, first = cut_of(FACTOR_CUTS, 2 * P * piece)
+            scale_rows = factor[c][:, 2 * pair : 2 * pair + 2, first : first + 2 * P]
+            if piece == 3:
+                for i in range(2):
+                    nc.gpsimd.tensor_tensor(h_rows[n][:, i, :], h_block[:, i, :], scale_rows[:, i, :], ALU.mult)
+            else:
+                nc.gpsimd.tensor_tensor(h_rows[n][:], h_block[:], scale_rows, ALU.mult)
+
+        def put(a, piece, t, h_rows):
+            entries = list_put[:, 16 * piece : 16 * (piece + 1)]
+            nc.vector.tensor_copy(page[a][t][:].indirect(entries), h_rows[:, t % 2, :])
 
         def fetch(a, t):
-            picked = ring.tile([P, NX], F32, name="picked")
-            nc.vector.tensor_copy(picked[:], page[a][t][:].indirect(list_get[:]))
-            nc.scalar.activation(x_bf[a][:, :, t], picked[:], ACT.Identity, bias=shift_sb[:, a, t : t + 1])
+            picked[a, t] = ring.tile([P, NX], F32, name="picked", bufs=4)
+            nc.vector.tensor_copy(picked[a, t][:], page[a][t][:].indirect(list_get[:]))
+
+        def add_shift(a, t):
+            nc.scalar.activation(x_bf[a][:, :, t], picked[a, t][:], ACT.Identity, bias=shift_sb[:, a, t : t + 1])
 
         def gather_v2():
+            v2_s[0] = kept([P, S2], U8, "v2_s")
+            nc.vector.tensor_copy(v2_s[0][:], tab2_s[:].indirect(list_v2[:]))
             for a in range(2):
+                v2_w[a] = kept([P, S2], U32, f"v2_w{a}")
                 nc.vector.tensor_copy(v2_w[a][:], tab2_w[a][:].bitcast(U32).indirect(list_v2[:]))
-            nc.vector.tensor_copy(v2_s[:], tab2_s[:].indirect(list_v2[:]))
 
-        gather_v(0)
-        interleave_wa(0, nc.vector.tensor_copy)
-        gather_v(1)
-        quantise(wa_w[0], wa_s[0], wa_bf[0])
-        interleave_wa(1, nc.scalar.copy)
+        for c in range(2):
+            gather_words(c)
+            gather_scales(c)
+        interleave_wa(0, nc.scalar.copy)
+        interleave_wa(1, nc.vector.tensor_copy)
+        quantise_wa(0)
+        quantise_wa(1)
+        gather_words(2, tag="wa_bf0")
 
         subj_sb = []
-        groups = [(a, jh) for a in range(2) for jh in range(2)]
-        h_rows = {}
-        h_rows[0] = ring.tile([P, PACK, HALF], F32, name="h_rows")
-        for jb in range(4):
-            features(0, 0, jb, h_rows[0])
-        for g, (a, jh) in enumerate(groups):
-            if g + 1 < len(groups):
-                h_rows[g + 1] = ring.tile([P, PACK, HALF], F32, name="h_rows")
-            if g == 1:
-                quantise(wa_w[1], wa_s[1], wa_bf[1])
-            if g == 2:
+        def place(n):
+            if n >= VECTOR_BLOCKS:
+                turn(n)
+            a, block = blocks[n]
+            for t in (2 * (block % 2), 2 * (block % 2) + 1):
+                put(a, block // 2, t, h_rows[n])
+                if block // 2 == 3:
+                    fetch(a, t)
+                    if a == 1:
+                        add_shift(a, t)
+
+        x_bf[1] = kept([P, NX, PACK], BF16, "x_bf1")
+        x_w[1] = kept([P, NX], U32, "x_w1")
+        maximum(0)
+        maximum(1)
+        minimum(0)
+        minimum(1)
+        turn(0)
+        turn(1)
+        gather_scales(2, tag="first_ya")
+        for n in range(2, 2 + LAG):
+            maximum(n)
+        for n in range(len(blocks)):
+            if n in (WA_AT + 1, WA_AT + 2):
+                wa_bf[n - WA_AT + 1] = kept([P, QUARTER, PACK], BF16, f"wa_bf{n - WA_AT + 1}")
+                interleave_wa(n - WA_AT + 1, nc.scalar.copy)
+            if n == WA_AT + 2:
+                quantise_wa(2)
+                quantise_wa(3)
+            if n == 9:
                 for i in range(2):
                     subj_sb.append(kept([P, 4, NX], F32, f"subj{i}", tag=f"wa_raw{i}"))
                     nc.sync.dma_start(out=subj_sb[i][:], in_=subj.rearrange("(i c p) n -> i p c n", i=2, p=P)[i])
-                quantise(x_w[0], x_s[0], x_bf[0])
                 gather_v2()
-            for t in range(PACK):
-                put(a, jh, t, h_rows[g])
-                if jh == 1:
-                    fetch(a, t)
-                if g + 1 < len(groups):
-                    features(*groups[g + 1], t, h_rows[g + 1])
-        quantise(x_w[1], x_s[1], x_bf[1])
+            if n + 2 + LAG < len(blocks):
+                maximum(n + 2 + LAG)
+            if n + 2 < len(blocks):
+                minimum(n + 2)
+            place(n)
+            if n == 9:
+                x_bf[0] = kept([P, NX, PACK], BF16, "x_bf0", tag="factor0")
+                for t in range(PACK):
+                    add_shift(0, t)
+            if n + 2 + LAG == len(blocks) - 1:
+                x_w[0] = kept([P, NX], U32, "x_w0", tag="wa_w1")
+                quantise(x_w[0][:], x_s[0][:], x_bf[0])
+        quantise(x_w[1][:], x_s[1][:], x_bf[1])
 
         tags = ("ya", "yb", "yc", "turned")
         scores = [psum.tile([P, NX], F32, name=f"score{m}", tag=tags[m % 4]) for m in range(S2 // P)]
@@ -210,13 +302,13 @@ def tile_list_catalogue_related_scores_kernel(
             for m in range(S2 // P):
                 cands = slice(P * m, P * (m + 1))
                 nc.tensor.matmul_mx(
-                    out=scores[m][:], lhsT=v2_w[a][:, cands].bitcast(FP8X4), lhsT_scale=v2_s[4 * a :, cands],
+                    out=scores[m][:], lhsT=v2_w[a][:, cands].bitcast(FP8X4), lhsT_scale=v2_s[0][4 * a :, cands],
                     rhs=x_w[a][:].bitcast(FP8X4), rhs_scale=x_s[a][:], start=(a == 0), stop=(a == 1),
                 )
         for m in range(S2 // P):
-            squashed = ring.tile([P, NX], F32, name="squashed", bufs=4)
-            weighted = ring.tile([P, NX], F32, name="weighted", bufs=4)
-            result = ring.tile([P, NX], F32, name="result", bufs=4)
+            squashed = step([P, NX], ("ya_sb", "larger")[m % 2])
+            weighted = step([P, NX], ("yc_sb", "room")[m % 2])
+            result = step([P, NX], ("excess", "h_block")[m % 2])
             nc.scalar.activation(squashed[:], scores[m][:], ACT.Tanh)
             nc.vector.tensor_tensor(weighted[:], squashed[:], subj_sb[m // 4][:, m % 4, :], ALU.mult)
             if m % 3 == 1:

@@ -19,16 +19,25 @@ ACT = mybir.ActivationFunctionType
 
 P = 128
 PACK = 4
-HALF = 512
-QUARTER = 256
-V_CUTS = (0, 256, 512, 1024)
-FACTOR_CUTS = (0, 256, 512, 1024)
-LAG = 2
-LARGER = 6
-HB = 3
-WA_AT = 2
-LATER = {WA_AT: "wa_bf2", WA_AT + 1: "wa_bf3", 5: "v2_s", 6: "v2_w0", 7: "v2_w1"}
-VECTOR_BLOCKS = 2
+HALF = P * PACK
+QUARTER = HALF // 2
+PER_COLUMN = 16
+QUADS, QUAD = 4, 32
+BLOCKS_PER_HALF = S // P
+BLOCKS = 2 * BLOCKS_PER_HALF
+OUT_TILES = S2 // P
+V_CUTS = (0, 256, 512, S)
+LEAD = 5
+DEPTH = 3
+SCALED_DEPTH = 5
+
+
+def minimum_on_vector(n):
+    return n < 4 or n == BLOCKS_PER_HALF
+
+
+def offset_on_scalar(m):
+    return OUT_TILES - 4 <= m < OUT_TILES - 1
 
 
 def tile_list_catalogue_related_scores_kernel(
@@ -38,280 +47,283 @@ def tile_list_catalogue_related_scores_kernel(
     nc = tc.nc
     with ExitStack() as ctx:
         keep = ctx.enter_context(tc.tile_pool(name="keep", bufs=1))
-        ring = ctx.enter_context(tc.tile_pool(name="ring", bufs=2))
+        ring = ctx.enter_context(tc.tile_pool(name="ring", bufs=DEPTH))
         psum = ctx.enter_context(tc.psum_pool(name="psum", bufs=2))
 
-        def kept(shape, dtype, name, tag=""):
-            return keep.tile(shape, dtype, name=name, tag=tag or name, align_bytes=64)
+        def kept(shape, dtype, name, after=""):
+            return keep.tile(shape, dtype, name=name, tag=after or name, align_bytes=64)
 
-        list_v = kept([P, S // 16], U16, "list_v")
-        list_v2 = kept([P, S2 // 16], U16, "list_v2")
-        list_put = kept([P, S // 16], U16, "list_put")
-        list_get = kept([P, NX // 16], U16, "list_get")
+        def passing(shape, tag):
+            return ring.tile(shape, F32, name=tag, tag=tag, bufs=SCALED_DEPTH if tag == "scaled" else DEPTH)
+
+        def shared_slot(n, shape, name):
+            return kept(shape, F32, name, after=f"slot{n % (LEAD + 1)}")
+
+        def shared_bank(n, shape, name):
+            return psum.tile(shape, F32, name=name, tag=f"bank{n % 4}", bufs=1)
+
+        list_v = kept([P, S // PER_COLUMN], U16, "list_v")
+        list_v2 = kept([P, S2 // PER_COLUMN], U16, "list_v2")
+        list_put = kept([P, S // PER_COLUMN], U16, "list_put")
+        list_get = kept([P, NX // PER_COLUMN], U16, "list_get")
         tab_w = kept([P, T], I32, "tab_w")
         tab_s = kept([P, T], U8, "tab_s")
-        tab2_w = [kept([P, T3], I32, f"tab2_w{a}") for a in range(2)]
+        tab2_w = {1: kept([P, T3], I32, "tab2_w1")}
         tab2_s = kept([P, T3], U8, "tab2_s")
         wa_raw = [kept([P, PACK, HALF], F32, f"wa_raw{a}") for a in range(2)]
-        wa_bf = {q: kept([P, QUARTER, PACK], BF16, f"wa_bf{q}") for q in range(2)}
-        wa_w = [kept([P, HALF], U32, f"wa_w{a}") for a in range(2)]
+        wa_first = [kept([P, QUARTER, PACK], BF16, f"wa_first{q}") for q in range(2)]
+        wa_w = [kept([P, HALF], U32, "wa_w0")]
         wa_s = [kept([P, HALF], U8, f"wa_s{a}") for a in range(2)]
         wb_w = [kept([P, HALF], I32, f"wb_w{a}") for a in range(2)]
         wc_w = [kept([P, 2 * HALF], U8, f"wc_w{a}") for a in range(2)]
         wb_s = kept([P, H], U8, "wb_s")
         wc_s = kept([P, H], U8, "wc_s")
-        factor = [kept([P, PACK, hi - lo], F32, f"factor{lo}") for lo, hi in zip(FACTOR_CUTS, FACTOR_CUTS[1:])]
+        wgs_sb = kept([P, S], F32, "wgs_sb")
+        factor = [kept([P, 2, PACK, QUADS, QUAD], F32, f"factor{i}") for i in range(BLOCKS_PER_HALF // 2)]
         page = [[kept([P, T2], F32, f"page{a}_{t}") for t in range(PACK)] for a in range(2)]
         shift_sb = kept([P, 2, PACK], F32, "shift_sb")
-        cand_sb = kept([P, S2 // P], F32, "cand_sb")
-        v_w = {}
-        v_s = {}
-        v2_w = {}
-        v2_s = {}
-        x_bf = {}
-        x_w = {}
+        cand_sb = kept([P, OUT_TILES], F32, "cand_sb")
         x_s = [kept([P, NX], U8, f"x_s{a}") for a in range(2)]
         ident = kept([P, P], F32, "ident")
+        v_w, v_s, v2_w, x_w = {}, {}, {}, {}
+        neg_larger, scaled, new_rows, picked = {}, {}, {}, {}
+        x_pairs, subj_sb = [], []
 
         def load_scale_rows(queue, plane, scales):
             passes = scales.shape[0]
-            for q in range(4):
+            for q in range(QUADS):
                 rows = scales[:, 4 * q : 4 * q + 4, :]
                 if passes == 1:
                     rows = rows[0]
-                queue.dma_start(out=plane[32 * q : 32 * q + 4 * passes, :].bitcast(I32), in_=rows.bitcast(I32))
+                queue.dma_start(out=plane[QUAD * q : QUAD * q + 4 * passes, :].bitcast(I32), in_=rows.bitcast(I32))
 
-        def words(dram, a, c0, c1):
-            return dram[a].rearrange("p c i -> p (c i)")[:, 4 * c0 : 4 * c1].bitcast(I32)
+        def words(dram, a, first, stop):
+            return dram[a].rearrange("p c i -> p (c i)")[:, PACK * first : PACK * stop].bitcast(I32)
 
         def load_weights(a):
-            cols = slice(HALF * a, HALF * (a + 1))
-            nc.sync.dma_start(out=wa_raw[a][:], in_=wa.rearrange("(p i) r -> p i r", i=PACK)[:, :, cols])
-            nc.sync.dma_start(out=wb_w[a][:], in_=words(wb_words, 0, cols.start, cols.stop))
-            nc.sync.dma_start(out=wc_w[a][:].bitcast(I32), in_=wc_words[0][:, 2 * cols.start : 2 * cols.stop].bitcast(I32))
-
-        def load_factor(c):
-            rows = wgs.rearrange("(q t) j -> q t j", t=PACK)[:, :, FACTOR_CUTS[c] : FACTOR_CUTS[c + 1]]
-            for quad in (0, 2, 1, 3):
-                nc.sync.dma_start(out=factor[c][32 * quad : 32 * (quad + 1)], in_=rows)
+            first, stop = HALF * a, HALF * (a + 1)
+            nc.sync.dma_start(out=wa_raw[a][:], in_=wa.rearrange("(p i) r -> p i r", i=PACK)[:, :, first:stop])
+            nc.sync.dma_start(out=wb_w[a][:], in_=words(wb_words, 0, first, stop))
+            nc.sync.dma_start(out=wc_w[a][:].bitcast(I32), in_=wc_words[0][:, 2 * first : 2 * stop].bitcast(I32))
 
         def load_page(a, t):
-            rows = page0.rearrange("(a p t) c -> a t p c", a=2, t=PACK)[a, t]
-            nc.sync.dma_start(out=page[a][t][:], in_=rows)
+            nc.sync.dma_start(out=page[a][t][:], in_=page0.rearrange("(a p t) c -> a t p c", a=2, t=PACK)[a, t])
 
         nc.vector.memset(tab_s[:].bitcast(I32), 0)
         nc.vector.memset(wb_s[:].bitcast(I32), 0)
-        nc.vector.memset(tab2_s[:].bitcast(I32), 0)
         nc.gpsimd.memset(wc_s[:].bitcast(I32), 0)
         nc.sync.dma_start(list_v[:], offs)
         nc.sync.dma_start(out=tab_w[:], in_=words(tab_words, 0, 0, T))
         load_scale_rows(nc.sync, tab_s, tab_scales)
         load_scale_rows(nc.gpsimd, wc_s, wc_scales)
         make_identity(nc, ident[:])
+        nc.gpsimd.memset(tab2_s[:].bitcast(I32), 0)
         load_weights(0)
         load_scale_rows(nc.sync, wb_s, wb_scales)
+        nc.sync.dma_start(out=wgs_sb[:], in_=wgs)
         load_page(0, 0)
         nc.sync.dma_start(list_put[:], offs3)
-        load_factor(0)
         for t in range(1, PACK):
             load_page(0, t)
-        load_factor(1)
-        load_factor(2)
         load_weights(1)
         nc.sync.dma_start(list_get[:], offs4)
-        with nc.allow_non_contiguous_dma(reason="small per-partition vectors"):
+        with nc.allow_non_contiguous_dma(reason="four values a partition and half"):
             nc.sync.dma_start(out=shift_sb[:], in_=shift.rearrange("(a p t) -> p a t", a=2, t=PACK))
-        nc.sync.dma_start(list_v2[:], offs2)
-        load_scale_rows(nc.sync, tab2_s, tab2_scales)
-        for a in range(2):
-            nc.sync.dma_start(out=tab2_w[a][:], in_=words(tab2_words, a, 0, T3))
         for t in range(PACK):
             load_page(1, t)
-        with nc.allow_non_contiguous_dma(reason="small per-partition vectors"):
+        nc.sync.dma_start(list_v2[:], offs2)
+        load_scale_rows(nc.sync, tab2_s, tab2_scales)
+        nc.sync.dma_start(out=tab2_w[1][:], in_=words(tab2_words, 1, 0, T3))
+        with nc.allow_non_contiguous_dma(reason="one value a partition and output tile"):
             nc.sync.dma_start(out=cand_sb[:], in_=cand.rearrange("(c p) -> p c", p=P))
 
-        def gather_words(c, tag=""):
-            v_w[c] = kept([P, V_CUTS[c + 1] - V_CUTS[c]], U32, f"v_w{c}", tag)
-            nc.vector.tensor_copy(v_w[c][:], tab_w[:].bitcast(U32).indirect(list_v[:, V_CUTS[c] // 16 : V_CUTS[c + 1] // 16]))
+        def entries(list_tile, first, stop):
+            return list_tile[:, first // PER_COLUMN : stop // PER_COLUMN]
 
-        def gather_scales(c, tag=""):
-            v_s[c] = kept([P, V_CUTS[c + 1] - V_CUTS[c]], U8, f"v_s{c}", tag)
-            nc.vector.tensor_copy(v_s[c][:], tab_s[:].indirect(list_v[:, V_CUTS[c] // 16 : V_CUTS[c + 1] // 16]))
+        def gather_v_words(c, after=""):
+            v_w[c] = kept([P, V_CUTS[c + 1] - V_CUTS[c]], U32, f"v_w{c}", after)
+            nc.vector.tensor_copy(v_w[c][:], tab_w[:].bitcast(U32).indirect(entries(list_v, V_CUTS[c], V_CUTS[c + 1])))
 
-        def interleave_wa(q, copy):
-            raw = wa_raw[q // 2][:, :, QUARTER * (q % 2) : QUARTER * (q % 2 + 1)]
-            copy(wa_bf[q][:].rearrange("p (c i) t -> p c t i", i=4), raw.rearrange("p t (c i) -> p c t i", i=4))
+        def gather_v_scales(c, after=""):
+            v_s[c] = kept([P, V_CUTS[c + 1] - V_CUTS[c]], U8, f"v_s{c}", after)
+            nc.vector.tensor_copy(v_s[c][:], tab_s[:].indirect(entries(list_v, V_CUTS[c], V_CUTS[c + 1])))
 
-        def quantise_wa(q):
-            cols = slice(QUARTER * (q % 2), QUARTER * (q % 2 + 1))
-            quantise(wa_w[q // 2][:, cols], wa_s[q // 2][:, cols], wa_bf[q])
+        def gather_v2_words(a, first, stop, after=""):
+            v2_w[a, first] = kept([P, stop - first], U32, f"v2_w{a}_{first}", after)
+            nc.vector.tensor_copy(v2_w[a, first][:], tab2_w[a][:].bitcast(U32).indirect(entries(list_v2, first, stop)))
 
-        def cut_of(cuts, entry):
-            c = max(i for i, lo in enumerate(cuts[:-1]) if lo <= entry)
-            return c, entry - cuts[c]
+        def interleave_wa(copy, grouped, a, q):
+            raw = wa_raw[a][:, :, QUARTER * q : QUARTER * (q + 1)]
+            copy(grouped.rearrange("p (c i) t -> p c t i", i=4), raw.rearrange("p t (c i) -> p c t i", i=4))
 
-        def quantise(codes, scales, values):
-            nc.vector.quantize_mx(out=codes.bitcast(FP8X4), scales=scales, in_=values[:].rearrange("p c t -> p (c t)"))
+        def quantise(codes, scales, grouped):
+            nc.vector.quantize_mx(out=codes.bitcast(FP8X4), scales=scales, in_=grouped[:].rearrange("p c t -> p (c t)"))
 
-        def step(shape, tag):
-            return ring.tile(shape, F32, name=tag, tag=tag, bufs={"larger": LARGER, "excess": 4, "h_rows": HB}.get(tag, 3))
-
-        def dealt(bank):
-            return bank[:].rearrange("p (m t) -> p t m", t=PACK)
-
-        blocks = [(a, block) for a in range(2) for block in range(S // P)]
-        terms = {}
-        picked = {}
-        neg_larger = {}
-        h_rows = {}
-
-        def product(n, tag, codes, scales):
-            c, first = cut_of(V_CUTS, P * blocks[n][1])
-            entries = slice(first, first + P)
-            bank = psum.tile([P, HALF], F32, name=tag, tag=tag)
+        def product(n, bank, codes, scales):
+            entry = P * (n % BLOCKS_PER_HALF)
+            c = max(i for i, first in enumerate(V_CUTS[:-1]) if first <= entry)
+            columns = slice(entry - V_CUTS[c], entry - V_CUTS[c] + P)
             nc.tensor.matmul_mx(
-                out=bank[:], lhsT=v_w[c][:, entries].bitcast(FP8X4), lhsT_scale=v_s[c][:, entries],
+                out=bank[:], lhsT=v_w[c][:, columns].bitcast(FP8X4), lhsT_scale=v_s[c][:, columns],
                 rhs=codes, rhs_scale=scales, start=True, stop=True,
             )
-            return dealt(bank)
+            return bank[:].rearrange("j (p t) -> j t p", t=PACK)
 
         def maximum(n):
-            a = blocks[n][0]
-            ya = product(n, "ya", wa_w[a][:].bitcast(FP8X4), wa_s[a][:])
-            yb = product(n, "yb", wb_w[a][:].bitcast(FP8X4), wb_s[:, HALF * a : HALF * (a + 1)])
-            neg_ya = kept([P, PACK, P], F32, "first_ya") if n == 1 else step([P, PACK, P], "ya_sb")
-            neg_larger[n] = step([P, PACK, P], "larger")
+            a = n // BLOCKS_PER_HALF
+            bank_a = shared_bank(n - 2, [P, HALF], "ya") if n in (2, 3) else psum.tile([P, HALF], F32, name="ya")
+            ya = product(n, bank_a, wa_w[a][:].bitcast(FP8X4), wa_s[a][:])
+            yb = product(n, shared_bank(n, [P, HALF], "yb"), wb_w[a][:].bitcast(FP8X4), wb_s[:, HALF * a : HALF * (a + 1)])
+            neg_ya = passing([P, PACK, P], "neg_ya")
+            if n == 0:
+                neg_larger[n] = kept([P, PACK, P], F32, "first_larger")
+            else:
+                neg_larger[n] = shared_slot(n, [P, PACK, P], "neg_larger")
             nc.scalar.activation(neg_ya[:], ya, ACT.Copy, scale=-1.0)
             nc.vector.scalar_tensor_tensor(neg_larger[n][:], yb, -1.0, neg_ya[:], ALU.mult, ALU.min)
 
         def minimum(n):
-            a = blocks[n][0]
-            yc = product(n, "turned" if n in (2, 3) else "yc", wc_w[a][:].bitcast(FP4X4), wc_s[:, HALF * a : HALF * (a + 1)])
-            excess = step([P, PACK, P], "excess")
-            if n < VECTOR_BLOCKS:
-                nc.vector.scalar_tensor_tensor(excess[:], yc, -1.0, neg_larger[n][:], ALU.mult, ALU.max)
-                terms[n] = [excess]
+            a, block = divmod(n, BLOCKS_PER_HALF)
+            yc = product(n, psum.tile([P, HALF], F32, name="yc"), wc_w[a][:].bitcast(FP4X4), wc_s[:, HALF * a : HALF * (a + 1)])
+            work = passing([P, PACK, P], "work")
+            if minimum_on_vector(n):
+                nc.vector.scalar_tensor_tensor(work[:], yc, -1.0, neg_larger[n][:], ALU.mult, ALU.max)
+                neg_h = work
             else:
-                yc_sb = step([P, PACK, P], "yc_sb")
-                room = step([P, PACK, P], "room")
+                yc_sb = passing([P, PACK, P], "yc_sb")
                 nc.scalar.copy(yc_sb[:], yc)
-                nc.gpsimd.tensor_tensor(room[:], yc_sb[:], neg_larger[n][:], ALU.add)
-                nc.scalar.activation(excess[:], room[:], ACT.Relu, scale=-1.0)
-                terms[n] = [neg_larger[n], excess]
+                nc.gpsimd.tensor_tensor(work[:], yc_sb[:], neg_larger[n][:], ALU.add)
+                nc.scalar.activation(work[:], work[:], ACT.Relu, scale=-1.0)
+                neg_h = yc_sb
+                nc.gpsimd.tensor_tensor(neg_h[:], work[:], neg_larger[n][:], ALU.add)
+            if n == BLOCKS_PER_HALF + 1:
+                scaled[n] = kept([P, PACK, P], F32, "x_pairs")
+            else:
+                scaled[n] = passing([P, PACK, P], "scaled")
+            factor_block = factor[block // 2][:, block % 2].rearrange("j t quad q -> j t (quad q)")
+            nc.gpsimd.tensor_tensor(scaled[n][:], neg_h[:], factor_block, ALU.mult)
 
         def turn(n):
-            a, block = blocks[n]
-            piece, pair = block // 2, block % 2
-            turned = psum.tile([P, 2, 2 * P], F32, name="turned", tag="turned")
-            passes = [(side, term, i) for side in range(2) for term in terms[n - pair + side] for i in range(2)]
-            for k, (side, term, i) in enumerate(passes):
-                nc.tensor.matmul(
-                    turned[:, i, P * side : P * (side + 1)], term[:, 2 * pair + i, :], ident[:], is_transpose=True,
-                    start=(k == 0), stop=(k == len(passes) - 1),
-                )
-            h_block = step([P, 2, 2 * P], "h_block")
-            nc.scalar.activation(h_block[:], turned[:], ACT.Copy, scale=-1.0)
-            h_rows[n] = kept([P, 2, 2 * P], F32, f"h_rows{n}", LATER[n]) if n in LATER else step([P, 2, 2 * P], "h_rows")
-            c, first = cut_of(FACTOR_CUTS, 2 * P * piece)
-            scale_rows = factor[c][:, 2 * pair : 2 * pair + 2, first : first + 2 * P]
-            if piece == 3:
+            first, pair = n - n % 2, n % 2
+            turned = shared_bank(n + 1, [P, 2, 2 * P], "turned")
+            for side in range(2):
                 for i in range(2):
-                    nc.gpsimd.tensor_tensor(h_rows[n][:, i, :], h_block[:, i, :], scale_rows[:, i, :], ALU.mult)
-            else:
-                nc.gpsimd.tensor_tensor(h_rows[n][:], h_block[:], scale_rows, ALU.mult)
+                    nc.tensor.transpose(turned[:, i, P * side : P * (side + 1)], scaled[first + side][:, 2 * pair + i, :], ident[:])
+            new_rows[n] = [shared_slot(n - 1, [P, 2 * P], "rows_even"), passing([P, 2 * P], "rows_odd")]
+            for i in range(2):
+                nc.scalar.activation(new_rows[n][i][:], turned[:, i, :], ACT.Copy, scale=-1.0)
 
-        def put(a, piece, t, h_rows):
-            entries = list_put[:, 16 * piece : 16 * (piece + 1)]
-            nc.vector.tensor_copy(page[a][t][:].indirect(entries), h_rows[:, t % 2, :])
-
-        def fetch(a, t):
-            picked[a, t] = ring.tile([P, NX], F32, name="picked", bufs=4)
-            nc.vector.tensor_copy(picked[a, t][:], page[a][t][:].indirect(list_get[:]))
+        def turn_factor(piece, tag):
+            turned = psum.tile([P, 2, P], F32, name="turned_factor", tag=tag)
+            for b in range(2):
+                nc.tensor.transpose(turned[:, b, :], wgs_sb[:, P * (2 * piece + b) : P * (2 * piece + b + 1)], ident[:])
+            by_row = turned[:].rearrange("j b (q t) -> j b t q", t=PACK).unsqueeze(3)
+            nc.scalar.copy(factor[piece][:], by_row.to_broadcast([P, 2, PACK, QUADS, QUAD]))
 
         def add_shift(a, t):
-            nc.scalar.activation(x_bf[a][:, :, t], picked[a, t][:], ACT.Identity, bias=shift_sb[:, a, t : t + 1])
+            nc.scalar.activation(x_pairs[a][:, t // 2, :, t % 2], picked[a, t][:], ACT.Identity, bias=shift_sb[:, a, t : t + 1])
 
-        def gather_v2():
-            v2_s[0] = kept([P, S2], U8, "v2_s")
-            nc.vector.tensor_copy(v2_s[0][:], tab2_s[:].indirect(list_v2[:]))
-            for a in range(2):
-                v2_w[a] = kept([P, S2], U32, f"v2_w{a}")
-                nc.vector.tensor_copy(v2_w[a][:], tab2_w[a][:].bitcast(U32).indirect(list_v2[:]))
+        def join_pairs(a, copy, word):
+            joined = x_bf[a][:].rearrange("p n t -> p (n t)").bitcast(word).rearrange("p (n w) -> p n w", w=2)
+            halves = x_pairs[a][:].rearrange("p w n e -> p w (n e)").bitcast(word).rearrange("p w n -> p n w")
+            copy(joined, halves)
 
-        for c in range(2):
-            gather_words(c)
-            gather_scales(c)
-        interleave_wa(0, nc.scalar.copy)
-        interleave_wa(1, nc.vector.tensor_copy)
-        quantise_wa(0)
-        quantise_wa(1)
-        gather_words(2, tag="wa_bf0")
-
-        subj_sb = []
         def place(n):
-            if n >= VECTOR_BLOCKS:
-                turn(n)
-            a, block = blocks[n]
-            for t in (2 * (block % 2), 2 * (block % 2) + 1):
-                put(a, block // 2, t, h_rows[n])
-                if block // 2 == 3:
-                    fetch(a, t)
+            a, block = divmod(n - n % 2, BLOCKS_PER_HALF)
+            for i in range(2):
+                t = 2 * (n % 2) + i
+                nc.vector.tensor_copy(page[a][t][:].indirect(entries(list_put, P * block, P * (block + 2))), new_rows[n][i][:])
+                if block + 2 == BLOCKS_PER_HALF:
+                    picked[a, t] = ring.tile([P, NX], F32, name="picked", bufs=PACK)
+                    nc.vector.tensor_copy(picked[a, t][:], page[a][t][:].indirect(list_get[:]))
                     if a == 1:
                         add_shift(a, t)
 
-        x_bf[1] = kept([P, NX, PACK], BF16, "x_bf1")
+        gather_v_words(0)
+        gather_v_scales(0)
+        gather_v_words(1)
+        gather_v_scales(1)
+        interleave_wa(nc.scalar.copy, wa_first[0][:], 0, 0)
+        interleave_wa(nc.vector.tensor_copy, wa_first[1][:], 0, 1)
+        for q in range(2):
+            quantise(wa_w[0][:, QUARTER * q : QUARTER * (q + 1)], wa_s[0][:, QUARTER * q : QUARTER * (q + 1)], wa_first[q])
+        gather_v_words(2, after="wa_first1")
+        tab2_w[0] = kept([P, T3], I32, "tab2_w0", after="tab_w")
+        nc.sync.dma_start(out=tab2_w[0][:], in_=words(tab2_words, 0, 0, T3))
+        x_bf = [kept([P, NX, PACK], BF16, f"x_bf{a}") for a in range(2)]
         x_w[1] = kept([P, NX], U32, "x_w1")
+
         maximum(0)
         maximum(1)
+        turn_factor(0, "ya")
         minimum(0)
         minimum(1)
+        maximum(2)
+        maximum(3)
+        gather_v_scales(2, after="first_larger")
+        turn_factor(1, "yc")
         turn(0)
         turn(1)
-        gather_scales(2, tag="first_ya")
-        for n in range(2, 2 + LAG):
-            maximum(n)
-        for n in range(len(blocks)):
-            if n in (WA_AT + 1, WA_AT + 2):
-                wa_bf[n - WA_AT + 1] = kept([P, QUARTER, PACK], BF16, f"wa_bf{n - WA_AT + 1}")
-                interleave_wa(n - WA_AT + 1, nc.scalar.copy)
-            if n == WA_AT + 2:
-                quantise_wa(2)
-                quantise_wa(3)
-            if n == 9:
-                for i in range(2):
-                    subj_sb.append(kept([P, 4, NX], F32, f"subj{i}", tag=f"wa_raw{i}"))
-                    nc.sync.dma_start(out=subj_sb[i][:], in_=subj.rearrange("(i c p) n -> i p c n", i=2, p=P)[i])
-                gather_v2()
-            if n + 2 + LAG < len(blocks):
-                maximum(n + 2 + LAG)
-            if n + 2 < len(blocks):
-                minimum(n + 2)
+        minimum(2)
+        minimum(3)
+        maximum(4)
+        turn_factor(2, "yc")
+
+        for n in range(BLOCKS):
+            if n >= 2:
+                turn(n)
             place(n)
-            if n == 9:
-                x_bf[0] = kept([P, NX, PACK], BF16, "x_bf0", tag="factor0")
+            if n + LEAD == BLOCKS_PER_HALF - 1:
+                wa_second = kept([P, HALF, PACK], BF16, "wa_second")
+                for q in range(2):
+                    interleave_wa(nc.scalar.copy, wa_second[:, QUARTER * q : QUARTER * (q + 1)], 1, q)
+                wa_w.append(kept([P, HALF], U32, "wa_w1"))
+                quantise(wa_w[1][:], wa_s[1][:], wa_second)
+            if n + LEAD < BLOCKS:
+                maximum(n + LEAD)
+            if n + LEAD - 1 == BLOCKS_PER_HALF - 2:
+                turn_factor(3, "yc")
+            if n + LEAD - 1 < BLOCKS:
+                minimum(n + LEAD - 1)
+            if n == BLOCKS_PER_HALF - 1:
+                for i in range(2):
+                    subj_sb.append(kept([P, OUT_TILES // 2, NX], F32, f"subj{i}", after=f"wa_raw{i}"))
+                    nc.sync.dma_start(out=subj_sb[i][:], in_=subj.rearrange("(i c p) n -> i p c n", i=2, p=P)[i])
+                v2_s = kept([P, S2], U8, "v2_s")
+                nc.vector.tensor_copy(v2_s[:], tab2_s[:].indirect(list_v2[:]))
+                gather_v2_words(0, 0, S2)
+            if n == BLOCKS_PER_HALF + 1:
+                x_pairs.append(kept([P, 2, NX, 2], BF16, "x_pairs0", after="x_pairs"))
                 for t in range(PACK):
                     add_shift(0, t)
-            if n + 2 + LAG == len(blocks) - 1:
-                x_w[0] = kept([P, NX], U32, "x_w0", tag="wa_w1")
+                join_pairs(0, nc.scalar.copy, U32)
+                x_pairs.append(kept([P, 2, NX, 2], BF16, "x_pairs1", after="x_pairs"))
+            if n + LEAD == BLOCKS:
+                x_w[0] = kept([P, NX], U32, "x_w0", after="factor3")
                 quantise(x_w[0][:], x_s[0][:], x_bf[0])
-        quantise(x_w[1][:], x_s[1][:], x_bf[1])
 
-        tags = ("ya", "yb", "yc", "turned")
-        scores = [psum.tile([P, NX], F32, name=f"score{m}", tag=tags[m % 4]) for m in range(S2 // P)]
+        gather_v2_words(1, 0, S2 // 2, after="page1_2")
+        join_pairs(1, nc.vector.tensor_copy, I32)
+        quantise(x_w[1][:], x_s[1][:], x_bf[1])
+        gather_v2_words(1, S2 // 2, S2, after="x_pairs")
+
+        scores = [shared_bank(m, [P, NX], f"score{m}") for m in range(4)]
+        scores = scores + [psum.tile([P, NX], F32, name=f"score{m}", tag=("ya", "yc")[m % 2]) for m in range(4, OUT_TILES)]
         for a in range(2):
-            for m in range(S2 // P):
-                cands = slice(P * m, P * (m + 1))
+            for m in range(OUT_TILES):
+                first = (S2 // 2) * (2 * m // OUT_TILES) if a == 1 else 0
                 nc.tensor.matmul_mx(
-                    out=scores[m][:], lhsT=v2_w[a][:, cands].bitcast(FP8X4), lhsT_scale=v2_s[0][4 * a :, cands],
+                    out=scores[m][:], lhsT=v2_w[a, first][:, P * m - first : P * (m + 1) - first].bitcast(FP8X4),
+                    lhsT_scale=v2_s[4 * a :, P * m : P * (m + 1)],
                     rhs=x_w[a][:].bitcast(FP8X4), rhs_scale=x_s[a][:], start=(a == 0), stop=(a == 1),
                 )
-        for m in range(S2 // P):
-            squashed = step([P, NX], ("ya_sb", "larger")[m % 2])
-            weighted = step([P, NX], ("yc_sb", "room")[m % 2])
-            result = step([P, NX], ("excess", "h_block")[m % 2])
+        for m in range(OUT_TILES):
+            squashed = passing([P, NX], ("neg_ya", "squashed")[m % 2])
+            weighted = passing([P, NX], ("yc_sb", "weighted")[m % 2])
+            result = passing([P, NX], ("scaled", "result")[m % 2])
             nc.scalar.activation(squashed[:], scores[m][:], ACT.Tanh)
-            nc.vector.tensor_tensor(weighted[:], squashed[:], subj_sb[m // 4][:, m % 4, :], ALU.mult)
-            if m % 3 == 1:
+            nc.vector.tensor_tensor(weighted[:], squashed[:], subj_sb[2 * m // OUT_TILES][:, m % (OUT_TILES // 2), :], ALU.mult)
+            if offset_on_scalar(m):
                 nc.scalar.activation(result[:], weighted[:], ACT.Identity, bias=cand_sb[:, m : m + 1])
             else:
                 nc.vector.tensor_scalar(result[:], weighted[:], cand_sb[:, m : m + 1], None, ALU.add)

from contextlib import ExitStack

import concourse.mybir as mybir
from concourse.masks import make_identity

K, H, T, S, T2, T3, S2, NX = 512, 1024, 2048, 1024, 2048, 2048, 1024, 512
FLOPS = 3 * 2 * K * H * S + 2 * H * S2 * NX

F32 = mybir.dt.float32
BF16 = mybir.dt.bfloat16
I32 = mybir.dt.int32
U32 = mybir.dt.uint32
U16 = mybir.dt.uint16
U8 = mybir.dt.uint8
FP8X4 = mybir.dt.float8_e4m3fn_x4
FP4X4 = mybir.dt.float4_e2m1fn_x4
ALU = mybir.AluOpType
ACT = mybir.ActivationFunctionType

P = 128
PACK = 4
HALF = P * PACK
QUARTER = HALF // 2
PER_COLUMN = 16
QUADS, QUAD = 4, 32
BLOCKS_PER_HALF = S // P
BLOCKS = 2 * BLOCKS_PER_HALF
OUT_TILES = S2 // P
V_CUTS = (0, 256, 512, S)
LEAD = 5
DEPTH = 3
SCALED_DEPTH = 5


def minimum_on_vector(n):
    return n < 4 or n == BLOCKS_PER_HALF


def offset_on_scalar(m):
    return OUT_TILES - 4 <= m < OUT_TILES - 1


def tile_list_catalogue_related_scores_kernel(
    tc, tab_words, tab_scales, tab2_words, tab2_scales, wa, wb_words, wb_scales, wc_words, wc_scales,
    wgs, page0, shift, subj, cand, offs, offs2, offs3, offs4, out,
):
    nc = tc.nc
    with ExitStack() as ctx:
        keep = ctx.enter_context(tc.tile_pool(name="keep", bufs=1))
        ring = ctx.enter_context(tc.tile_pool(name="ring", bufs=DEPTH))
        psum = ctx.enter_context(tc.psum_pool(name="psum", bufs=2))

        def kept(shape, dtype, name, after=""):
            return keep.tile(shape, dtype, name=name, tag=after or name, align_bytes=64)

        def passing(shape, tag):
            return ring.tile(shape, F32, name=tag, tag=tag, bufs=SCALED_DEPTH if tag == "scaled" else DEPTH)

        def shared_slot(n, shape, name):
            return kept(shape, F32, name, after=f"slot{n % (LEAD + 1)}")

        def shared_bank(n, shape, name):
            return psum.tile(shape, F32, name=name, tag=f"bank{n % 4}", bufs=1)

        list_v = kept([P, S // PER_COLUMN], U16, "list_v")
        list_v2 = kept([P, S2 // PER_COLUMN], U16, "list_v2")
        list_put = kept([P, S // PER_COLUMN], U16, "list_put")
        list_get = kept([P, NX // PER_COLUMN], U16, "list_get")
        tab_w = kept([P, T], I32, "tab_w")
        tab_s = kept([P, T], U8, "tab_s")
        tab2_w = {1: kept([P, T3], I32, "tab2_w1")}
        tab2_s = kept([P, T3], U8, "tab2_s")
        wa_raw = [kept([P, PACK, HALF], F32, f"wa_raw{a}") for a in range(2)]
        wa_first = [kept([P, QUARTER, PACK], BF16, f"wa_first{q}") for q in range(2)]
        wa_w = [kept([P, HALF], U32, "wa_w0")]
        wa_s = [kept([P, HALF], U8, f"wa_s{a}") for a in range(2)]
        wb_w = [kept([P, HALF], I32, f"wb_w{a}") for a in range(2)]
        wc_w = [kept([P, 2 * HALF], U8, f"wc_w{a}") for a in range(2)]
        wb_s = kept([P, H], U8, "wb_s")
        wc_s = kept([P, H], U8, "wc_s")
        wgs_sb = kept([P, S], F32, "wgs_sb")
        factor = [kept([P, 2, PACK, QUADS, QUAD], F32, f"factor{i}") for i in range(BLOCKS_PER_HALF // 2)]
        page = [[kept([P, T2], F32, f"page{a}_{t}") for t in range(PACK)] for a in range(2)]
        shift_sb = kept([P, 2, PACK], F32, "shift_sb")
        cand_sb = kept([P, OUT_TILES], F32, "cand_sb")
        x_s = [kept([P, NX], U8, f"x_s{a}") for a in range(2)]
        ident = kept([P, P], F32, "ident")
        v_w, v_s, v2_w, x_w = {}, {}, {}, {}
        neg_larger, scaled, new_rows, picked = {}, {}, {}, {}
        x_pairs, subj_sb = [], []

        def load_scale_rows(queue, plane, scales):
            passes = scales.shape[0]
            for q in range(QUADS):
                rows = scales[:, 4 * q : 4 * q + 4, :]
                if passes == 1:
                    rows = rows[0]
                queue.dma_start(out=plane[QUAD * q : QUAD * q + 4 * passes, :].bitcast(I32), in_=rows.bitcast(I32))

        def words(dram, a, first, stop):
            return dram[a].rearrange("p c i -> p (c i)")[:, PACK * first : PACK * stop].bitcast(I32)

        def load_weights(a):
            first, stop = HALF * a, HALF * (a + 1)
            nc.sync.dma_start(out=wa_raw[a][:], in_=wa.rearrange("(p i) r -> p i r", i=PACK)[:, :, first:stop])
            nc.sync.dma_start(out=wb_w[a][:], in_=words(wb_words, 0, first, stop))
            nc.sync.dma_start(out=wc_w[a][:].bitcast(I32), in_=wc_words[0][:, 2 * first : 2 * stop].bitcast(I32))

        def load_page(a, t):
            nc.sync.dma_start(out=page[a][t][:], in_=page0.rearrange("(a p t) c -> a t p c", a=2, t=PACK)[a, t])

        nc.vector.memset(tab_s[:].bitcast(I32), 0)
        nc.vector.memset(wb_s[:].bitcast(I32), 0)
        nc.gpsimd.memset(wc_s[:].bitcast(I32), 0)
        nc.sync.dma_start(list_v[:], offs)
        nc.sync.dma_start(out=tab_w[:], in_=words(tab_words, 0, 0, T))
        load_scale_rows(nc.sync, tab_s, tab_scales)
        load_scale_rows(nc.gpsimd, wc_s, wc_scales)
        make_identity(nc, ident[:])
        nc.gpsimd.memset(tab2_s[:].bitcast(I32), 0)
        load_weights(0)
        load_scale_rows(nc.sync, wb_s, wb_scales)
        nc.sync.dma_start(out=wgs_sb[:], in_=wgs)
        load_page(0, 0)
        nc.sync.dma_start(list_put[:], offs3)
        for t in range(1, PACK):
            load_page(0, t)
        load_weights(1)
        nc.sync.dma_start(list_get[:], offs4)
        with nc.allow_non_contiguous_dma(reason="four values a partition and half"):
            nc.sync.dma_start(out=shift_sb[:], in_=shift.rearrange("(a p t) -> p a t", a=2, t=PACK))
        for t in range(PACK):
            load_page(1, t)
        nc.sync.dma_start(list_v2[:], offs2)
        load_scale_rows(nc.sync, tab2_s, tab2_scales)
        nc.sync.dma_start(out=tab2_w[1][:], in_=words(tab2_words, 1, 0, T3))
        with nc.allow_non_contiguous_dma(reason="one value a partition and output tile"):
            nc.sync.dma_start(out=cand_sb[:], in_=cand.rearrange("(c p) -> p c", p=P))

        def entries(list_tile, first, stop):
            return list_tile[:, first // PER_COLUMN : stop // PER_COLUMN]

        def gather_v_words(c, after=""):
            v_w[c] = kept([P, V_CUTS[c + 1] - V_CUTS[c]], U32, f"v_w{c}", after)
            nc.vector.tensor_copy(v_w[c][:], tab_w[:].bitcast(U32).indirect(entries(list_v, V_CUTS[c], V_CUTS[c + 1])))

        def gather_v_scales(c, after=""):
            v_s[c] = kept([P, V_CUTS[c + 1] - V_CUTS[c]], U8, f"v_s{c}", after)
            nc.vector.tensor_copy(v_s[c][:], tab_s[:].indirect(entries(list_v, V_CUTS[c], V_CUTS[c + 1])))

        def gather_v2_words(a, first, stop, after=""):
            v2_w[a, first] = kept([P, stop - first], U32, f"v2_w{a}_{first}", after)
            nc.vector.tensor_copy(v2_w[a, first][:], tab2_w[a][:].bitcast(U32).indirect(entries(list_v2, first, stop)))

        def interleave_wa(copy, grouped, a, q):
            raw = wa_raw[a][:, :, QUARTER * q : QUARTER * (q + 1)]
            copy(grouped.rearrange("p (c i) t -> p c t i", i=4), raw.rearrange("p t (c i) -> p c t i", i=4))

        def quantise(codes, scales, grouped):
            nc.vector.quantize_mx(out=codes.bitcast(FP8X4), scales=scales, in_=grouped[:].rearrange("p c t -> p (c t)"))

        def product(n, bank, codes, scales):
            entry = P * (n % BLOCKS_PER_HALF)
            c = max(i for i, first in enumerate(V_CUTS[:-1]) if first <= entry)
            columns = slice(entry - V_CUTS[c], entry - V_CUTS[c] + P)
            nc.tensor.matmul_mx(
                out=bank[:], lhsT=v_w[c][:, columns].bitcast(FP8X4), lhsT_scale=v_s[c][:, columns],
                rhs=codes, rhs_scale=scales, start=True, stop=True,
            )
            return bank[:].rearrange("j (p t) -> j t p", t=PACK)

        def maximum(n):
            a = n // BLOCKS_PER_HALF
            bank_a = shared_bank(n - 2, [P, HALF], "ya") if n in (2, 3) else psum.tile([P, HALF], F32, name="ya")
            ya = product(n, bank_a, wa_w[a][:].bitcast(FP8X4), wa_s[a][:])
            yb = product(n, shared_bank(n, [P, HALF], "yb"), wb_w[a][:].bitcast(FP8X4), wb_s[:, HALF * a : HALF * (a + 1)])
            neg_ya = passing([P, PACK, P], "neg_ya")
            if n == 0:
                neg_larger[n] = kept([P, PACK, P], F32, "first_larger")
            else:
                neg_larger[n] = shared_slot(n, [P, PACK, P], "neg_larger")
            nc.scalar.activation(neg_ya[:], ya, ACT.Copy, scale=-1.0)
            nc.vector.scalar_tensor_tensor(neg_larger[n][:], yb, -1.0, neg_ya[:], ALU.mult, ALU.min)

        def minimum(n):
            a, block = divmod(n, BLOCKS_PER_HALF)
            yc = product(n, psum.tile([P, HALF], F32, name="yc"), wc_w[a][:].bitcast(FP4X4), wc_s[:, HALF * a : HALF * (a + 1)])
            work = passing([P, PACK, P], "work")
            if minimum_on_vector(n):
                nc.vector.scalar_tensor_tensor(work[:], yc, -1.0, neg_larger[n][:], ALU.mult, ALU.max)
                neg_h = work
            else:
                yc_sb = passing([P, PACK, P], "yc_sb")
                nc.scalar.copy(yc_sb[:], yc)
                nc.gpsimd.tensor_tensor(work[:], yc_sb[:], neg_larger[n][:], ALU.add)
                nc.scalar.activation(work[:], work[:], ACT.Relu, scale=-1.0)
                neg_h = yc_sb
                nc.gpsimd.tensor_tensor(neg_h[:], work[:], neg_larger[n][:], ALU.add)
            if n == BLOCKS_PER_HALF + 1:
                scaled[n] = kept([P, PACK, P], F32, "x_pairs")
            else:
                scaled[n] = passing([P, PACK, P], "scaled")
            factor_block = factor[block // 2][:, block % 2].rearrange("j t quad q -> j t (quad q)")
            nc.gpsimd.tensor_tensor(scaled[n][:], neg_h[:], factor_block, ALU.mult)

        def turn(n):
            first, pair = n - n % 2, n % 2
            turned = shared_bank(n + 1, [P, 2, 2 * P], "turned")
            for side in range(2):
                for i in range(2):
                    nc.tensor.transpose(turned[:, i, P * side : P * (side + 1)], scaled[first + side][:, 2 * pair + i, :], ident[:])
            new_rows[n] = [shared_slot(n - 1, [P, 2 * P], "rows_even"), passing([P, 2 * P], "rows_odd")]
            for i in range(2):
                nc.scalar.activation(new_rows[n][i][:], turned[:, i, :], ACT.Copy, scale=-1.0)

        def turn_factor(piece, tag):
            turned = psum.tile([P, 2, P], F32, name="turned_factor", tag=tag)
            for b in range(2):
                nc.tensor.transpose(turned[:, b, :], wgs_sb[:, P * (2 * piece + b) : P * (2 * piece + b + 1)], ident[:])
            by_row = turned[:].rearrange("j b (q t) -> j b t q", t=PACK).unsqueeze(3)
            nc.scalar.copy(factor[piece][:], by_row.to_broadcast([P, 2, PACK, QUADS, QUAD]))

        def add_shift(a, t):
            nc.scalar.activation(x_pairs[a][:, t // 2, :, t % 2], picked[a, t][:], ACT.Identity, bias=shift_sb[:, a, t : t + 1])

        def join_pairs(a, copy, word):
            joined = x_bf[a][:].rearrange("p n t -> p (n t)").bitcast(word).rearrange("p (n w) -> p n w", w=2)
            halves = x_pairs[a][:].rearrange("p w n e -> p w (n e)").bitcast(word).rearrange("p w n -> p n w")
            copy(joined, halves)

        def place(n):
            a, block = divmod(n - n % 2, BLOCKS_PER_HALF)
            for i in range(2):
                t = 2 * (n % 2) + i
                nc.vector.tensor_copy(page[a][t][:].indirect(entries(list_put, P * block, P * (block + 2))), new_rows[n][i][:])
                if block + 2 == BLOCKS_PER_HALF:
                    picked[a, t] = ring.tile([P, NX], F32, name="picked", bufs=PACK)
                    nc.vector.tensor_copy(picked[a, t][:], page[a][t][:].indirect(list_get[:]))
                    if a == 1:
                        add_shift(a, t)

        gather_v_words(0)
        gather_v_scales(0)
        gather_v_words(1)
        gather_v_scales(1)
        interleave_wa(nc.scalar.copy, wa_first[0][:], 0, 0)
        interleave_wa(nc.vector.tensor_copy, wa_first[1][:], 0, 1)
        for q in range(2):
            quantise(wa_w[0][:, QUARTER * q : QUARTER * (q + 1)], wa_s[0][:, QUARTER * q : QUARTER * (q + 1)], wa_first[q])
        gather_v_words(2, after="wa_first1")
        tab2_w[0] = kept([P, T3], I32, "tab2_w0", after="tab_w")
        nc.sync.dma_start(out=tab2_w[0][:], in_=words(tab2_words, 0, 0, T3))
        x_bf = [kept([P, NX, PACK], BF16, f"x_bf{a}") for a in range(2)]
        x_w[1] = kept([P, NX], U32, "x_w1")

        maximum(0)
        maximum(1)
        turn_factor(0, "ya")
        minimum(0)
        minimum(1)
        maximum(2)
        maximum(3)
        gather_v_scales(2, after="first_larger")
        turn_factor(1, "yc")
        turn(0)
        turn(1)
        minimum(2)
        minimum(3)
        maximum(4)
        turn_factor(2, "yc")

        for n in range(BLOCKS):
            if n >= 2:
                turn(n)
            place(n)
            if n + LEAD == BLOCKS_PER_HALF - 1:
                wa_second = kept([P, HALF, PACK], BF16, "wa_second")
                for q in range(2):
                    interleave_wa(nc.scalar.copy, wa_second[:, QUARTER * q : QUARTER * (q + 1)], 1, q)
                wa_w.append(kept([P, HALF], U32, "wa_w1"))
                quantise(wa_w[1][:], wa_s[1][:], wa_second)
            if n + LEAD < BLOCKS:
                maximum(n + LEAD)
            if n + LEAD - 1 == BLOCKS_PER_HALF - 2:
                turn_factor(3, "yc")
            if n + LEAD - 1 < BLOCKS:
                minimum(n + LEAD - 1)
            if n == BLOCKS_PER_HALF - 1:
                for i in range(2):
                    subj_sb.append(kept([P, OUT_TILES // 2, NX], F32, f"subj{i}", after=f"wa_raw{i}"))
                    nc.sync.dma_start(out=subj_sb[i][:], in_=subj.rearrange("(i c p) n -> i p c n", i=2, p=P)[i])
                v2_s = kept([P, S2], U8, "v2_s")
                nc.vector.tensor_copy(v2_s[:], tab2_s[:].indirect(list_v2[:]))
                gather_v2_words(0, 0, S2)
            if n == BLOCKS_PER_HALF + 1:
                x_pairs.append(kept([P, 2, NX, 2], BF16, "x_pairs0", after="x_pairs"))
                for t in range(PACK):
                    add_shift(0, t)
                join_pairs(0, nc.scalar.copy, U32)
                x_pairs.append(kept([P, 2, NX, 2], BF16, "x_pairs1", after="x_pairs"))
            if n + LEAD == BLOCKS:
                x_w[0] = kept([P, NX], U32, "x_w0", after="factor3")
                quantise(x_w[0][:], x_s[0][:], x_bf[0])

        gather_v2_words(1, 0, S2 // 2, after="page1_2")
        join_pairs(1, nc.vector.tensor_copy, I32)
        quantise(x_w[1][:], x_s[1][:], x_bf[1])
        gather_v2_words(1, S2 // 2, S2, after="x_pairs")

        scores = [shared_bank(m, [P, NX], f"score{m}") for m in range(4)]
        scores = scores + [psum.tile([P, NX], F32, name=f"score{m}", tag=("ya", "yc")[m % 2]) for m in range(4, OUT_TILES)]
        for a in range(2):
            for m in range(OUT_TILES):
                first = (S2 // 2) * (2 * m // OUT_TILES) if a == 1 else 0
                nc.tensor.matmul_mx(
                    out=scores[m][:], lhsT=v2_w[a, first][:, P * m - first : P * (m + 1) - first].bitcast(FP8X4),
                    lhsT_scale=v2_s[4 * a :, P * m : P * (m + 1)],
                    rhs=x_w[a][:].bitcast(FP8X4), rhs_scale=x_s[a][:], start=(a == 0), stop=(a == 1),
                )
        for m in range(OUT_TILES):
            squashed = passing([P, NX], ("neg_ya", "squashed")[m % 2])
            weighted = passing([P, NX], ("yc_sb", "weighted")[m % 2])
            result = passing([P, NX], ("scaled", "result")[m % 2])
            nc.scalar.activation(squashed[:], scores[m][:], ACT.Tanh)
            nc.vector.tensor_tensor(weighted[:], squashed[:], subj_sb[2 * m // OUT_TILES][:, m % (OUT_TILES // 2), :], ALU.mult)
            if offset_on_scalar(m):
                nc.scalar.activation(result[:], weighted[:], ACT.Identity, bias=cand_sb[:, m : m + 1])
            else:
                nc.vector.tensor_scalar(result[:], weighted[:], cand_sb[:, m : m + 1], None, ALU.add)
            nc.sync.dma_start(out=out[P * m : P * (m + 1), :], in_=result[:])
